import numpy as np, ml_dtypes
CORES = [113,118,241,246]
N = 4
import mx_ref
NC, G, GR = 256, 4, 2
C = np.float32(0.041)
BF = ml_dtypes.bfloat16
def cut(t, i, w=512):
    return t[:, w * i:w * i + w]
def tile(rs):
    return np.stack(rs, axis=2).reshape(128, -1).astype(BF)
def layer(w, X):
    out = []
    for i in range(G):
        for t in range(len(X)):
            p = mx_ref.matmul(mx_ref.quantize(cut(w, len(X) * i + t)), X[t])
            z = p if t == 0 else z + p
        out.append(z)
    return out
def act(Z):
    return [np.maximum(z, 0) * C for z in Z]
def setup_inputs(rng):
    def f(*shape):
        return mx_ref.flush((rng.standard_normal(shape, dtype=np.float32) * np.exp2(rng.integers(-2, 3, shape[:-1] + (1,)))).astype(BF))
    return {"xa": f(N, 128, 512), "xb": f(N, 128, 4 * NC), "wa": f(N, 128, G * 512), "wb": f(N, 128, G * 512)}
def setup_inputs_blocks(rng):
    d = setup_inputs(rng)
    for k in ("xa", "xb", "wa", "wb"): d[k] = mx_ref.spread(d[k], rng, 2)
    return d
def setup_inputs_wide(rng):
    d = setup_inputs(rng)
    for k in ("xa", "xb", "wa", "wb"): d[k] = mx_ref.flush((d[k].astype(np.float32) * np.exp2(rng.integers(-5, 6, (N, 1, 1))).astype(np.float32)).astype(BF))
    return d
def reference(xa, xb, wa, wb):
    A = [mx_ref.quantize(tile(act(layer(wa[j], [mx_ref.quantize(xa[j])])))) for j in range(N)]
    M = [mx_ref.quantize(tile(act(layer(wb[j], [mx_ref.quantize(xb[j])])))) for j in range(N)]
    y = np.zeros((N, 128, NC), np.float32)
    for r in range(N):
        i, j = divmod(r, GR)
        for k in range(GR):
            p = mx_ref.matmul(A[GR * i + k], M[GR * k + j])
            y[r] = p if k == 0 else y[r] + p
    return {"y": y}

@@ -1,0 +1,108 @@
+from concourse.mybir import AluOpType, ActivationFunctionType, dt
+
+CODE, PLANE = "float8_e4m3fn_x4", "uint8"
+C = 0.041
+G = 4
+A, B = 128, 256
+
+SCRATCH = {
+    "xa_s": ("sbuf", [128, 4 * A], "bfloat16"), "xb_s": ("sbuf", [128, 4 * B], "bfloat16"),
+    "wa_s": ("sbuf", [128, G * 512], "bfloat16"), "wb_s": ("sbuf", [128, G * 512], "bfloat16"),
+    "ta": ("sbuf", [128, 4 * A], "bfloat16"), "tb": ("sbuf", [128, 4 * B], "bfloat16"),
+    "y_s": ("sbuf", [128, B], "float32"),
+    "cxa": ("sbuf", [128, A], CODE), "pxa": ("sbuf", [128, A], PLANE),
+    "cxb": ("sbuf", [128, B], CODE), "pxb": ("sbuf", [128, B], PLANE),
+    "cwa": ("sbuf", [128, G * 128], CODE), "pwa": ("sbuf", [128, G * 128], PLANE),
+    "cwb": ("sbuf", [128, G * 128], CODE), "pwb": ("sbuf", [128, G * 128], PLANE),
+    "ca": ("sbuf", [128, A], CODE), "pa": ("sbuf", [128, A], PLANE),
+    "cb": ("sbuf", [128, B], CODE), "pb": ("sbuf", [128, B], PLANE),
+    "cra": ("sbuf", [128, A], CODE), "pra": ("sbuf", [128, A], PLANE),
+    "crb": ("sbuf", [128, B], CODE), "prb": ("sbuf", [128, B], PLANE),
+}
+for _i in range(G):
+    SCRATCH["zb%d" % _i] = ("psum", [128, 512], "float32")
+    SCRATCH["za%d" % _i] = ("psum", [128, 512], "float32")
+
+SEMAPHORES = ["l_xa", "l_xb", "l_wa0", "l_wa1", "l_wb0", "l_wb1", "q_xa", "q_xb", "q_a", "q_b",
+              "arr_a", "arr_b", "sent", "y0", "y1", "yv", "ys", "stored"]
+SEMAPHORES += ["%s%d" % (n, i) for n in ("q_wa", "q_wb", "m_a", "m_b", "r_a", "r_b") for i in range(G)]
+
+
+def rank_program(g, core, T, topo):
+    rank = T.rank_of(core)
+    if rank is None:
+        return
+    S = T.sem
+    i, j = divmod(rank, 2)
+    row_peer = T.cores[2 * i + (1 - j)]
+    col_peer = T.cores[2 * (1 - i) + j]
+    Relu, Copy = ActivationFunctionType.Relu, ActivationFunctionType.Copy
+    cut = 3 * 512
+
+    g.sync.dma_start(T.xb_s[:], T.xb[:]).then_inc(S.l_xb, 16)
+    g.scalar.dma_start(T.wb_s[:, :cut], T.wb[:, :cut]).then_inc(S.l_wb0, 16)
+    g.sync.dma_start(T.wb_s[:, cut:], T.wb[:, cut:]).then_inc(S.l_wb1, 16)
+    g.scalar.dma_start(T.wa_s[:, :cut], T.wa[:, :cut]).then_inc(S.l_wa0, 16)
+    g.sync.dma_start(T.xa_s[:], T.xa[:]).then_inc(S.l_xa, 16)
+    g.sync.dma_start(T.wa_s[:, cut:], T.wa[:, cut:]).then_inc(S.l_wa1, 16)
+
+    for t, n in (("b", B), ("a", A)):
+        x, w, cx, px = T["x%s_s" % t], T["w%s_s" % t], T["cx" + t], T["px" + t]
+        cw, pw, h = T["cw" + t], T["pw" + t], T["t" + t]
+        g.vector.wait_ge(S["l_x" + t], 16)
+        g.vector.quantize_mx(cx[:], px[:], x[:]).then_inc(S["q_x" + t], 1)
+        g.tensor.wait_ge(S["q_x" + t], 1)
+        for b in range(G):
+            if b == 0:
+                g.vector.wait_ge(S["l_w%s0" % t], 16)
+            if b == G - 1:
+                g.vector.wait_ge(S["l_w%s1" % t], 16)
+            c = slice(128 * b, 128 * b + 128)
+            g.vector.quantize_mx(cw[:, c], pw[:, c], w[:, 512 * b:512 * b + 512]).then_inc(S["q_w%s%d" % (t, b)], 1)
+            z = T["z%s%d" % (t, b)]
+            g.tensor.wait_ge(S["q_w%s%d" % (t, b)], 1)
+            g.tensor.matmul_mx(z[:, :n], cw[:, c], pw[:, c], cx[:], px[:], True, True).then_inc(S["m_%s%d" % (t, b)], 1)
+            if b < G - 1:
+                g.scalar.wait_ge(S["m_%s%d" % (t, b)], 1)
+                g.scalar.activation(h[:, b:4 * n:4], z[:, :n], Relu, scale=C).then_inc(S["r_%s%d" % (t, b)], 1)
+            else:
+                g.vector.wait_ge(S["m_%s%d" % (t, b)], 1)
+                g.vector.tensor_scalar(h[:, b:4 * n:4], z[:, :n], 0.0, C, AluOpType.max, AluOpType.mult).then_inc(
+                    S["r_%s%d" % (t, b)], 1)
+        for b in range(G):
+            g.vector.wait_ge(S["r_%s%d" % (t, b)], 1)
+        g.vector.quantize_mx(T["c" + t][:], T["p" + t][:], h[:]).then_inc(S["q_" + t], 1)
+
+    eng_b = topo.mask(core, col_peer)
+    eng_a = topo.mask(core, row_peer) & eng_b
+    n_a, n_b = bin(eng_a).count("1"), bin(eng_b).count("1")
+    for t, dst, eng in (("b", col_peer, eng_b), ("a", row_peer, eng_a)):
+        rid, pid = topo.addr(dst, core)
+        g.wait_ge(S["q_" + t], 1)
+        g.remote_dma(T["cr" + t][:].bitcast(dt.uint8), T["c" + t][:].bitcast(dt.uint8), S["arr_" + t], S.sent, pid, rid, eng)
+        g.remote_dma(T["pr" + t][:], T["p" + t][:], S["arr_" + t], S.sent, pid, rid, eng)
+
+    own_a, rem_a = (T.ca, T.pa), (T.cra, T.pra)
+    own_b, rem_b = (T.cb, T.pb), (T.crb, T.prb)
+    slices = ((own_a, own_b), (rem_a, rem_b)) if i == j else ((own_a, rem_b), (rem_a, own_b))
+    g.tensor.wait_ge(S.q_b, 1)
+    g.tensor.wait_ge(S.q_a, 1)
+    for k, (a, b) in enumerate(slices):
+        if b is rem_b:
+            g.tensor.wait_ge(S.arr_b, 2 * n_b)
+        if a is rem_a:
+            g.tensor.wait_ge(S.arr_a, 2 * n_a)
+        for h in range(2):
+            c = slice(128 * h, 128 * h + 128)
+            mm = g.tensor.matmul_mx(T["zb%d" % h][:, :128], a[0][:], a[1][:], b[0][:, c], b[1][:, c], k == 0, k == 1)
+            if k == 1:
+                mm.then_inc(S["y%d" % h], 1)
+    g.vector.wait_ge(S.y0, 1)
+    g.vector.tensor_copy(T.y_s[:, :128], T.zb0[:, :128]).then_inc(S.yv, 1)
+    g.scalar.wait_ge(S.y1, 1)
+    g.scalar.activation(T.y_s[:, 128:], T.zb1[:, :128], Copy).then_inc(S.ys, 1)
+    g.sync.wait_ge(S.yv, 1)
+    g.sync.wait_ge(S.ys, 1)
+    g.sync.dma_start(T.y[:], T.y_s[:]).then_inc(S.stored, 16)
+    g.sync.wait_ge(S.stored, 16)
+    g.wait_ge(S.sent, 2 * n_a + 2 * n_b)

@@ -1,14 +1,22 @@
-from concourse.mybir import AluOpType, ActivationFunctionType, dt
+from concourse.mybir import ActivationFunctionType, dt
 
 CODE, PLANE = "float8_e4m3fn_x4", "uint8"
 C = 0.041
 G = 4
-A, B = 128, 256
+A, B, H = 128, 256, 128
+PIECES = {"xa": (0, 1), "xb": (0, 1, 2), "wa": (0, 1, 3, 4), "wb": (0, 2, 3, 4)}
+LOADS = (("sync", "xb", 0), ("scalar", "wb", 0), ("sync", "wb", 1), ("scalar", "wb", 2), ("sync", "xb", 1),
+         ("scalar", "xa", 0), ("sync", "wa", 0), ("scalar", "wa", 1), ("sync", "wa", 2))
+ORDER = (("xb", 0), ("wb", 0), ("wb", 1), ("wb", 2), ("wb", 3), ("xb", 1), ("b", 0), ("xa", 0), ("wa", 0), ("b", 1),
+         ("wa", 1), ("wa", 2), ("wa", 3), ("a", 0))
+PRODUCTS = (("b", 0, 0, 0), ("b", 1, 0, 1), ("b", 2, 0, 2), ("b", 3, 0, 3),
+            ("b", 0, 1, 4), ("b", 1, 1, 5), ("b", 2, 1, 6), ("b", 3, 1, 7),
+            ("a", 0, 0, 0), ("a", 1, 0, 1), ("a", 2, 0, 2), ("a", 3, 0, 3))
 
 SCRATCH = {
     "xa_s": ("sbuf", [128, 4 * A], "bfloat16"), "xb_s": ("sbuf", [128, 4 * B], "bfloat16"),
     "wa_s": ("sbuf", [128, G * 512], "bfloat16"), "wb_s": ("sbuf", [128, G * 512], "bfloat16"),
-    "ta": ("sbuf", [128, 4 * A], "bfloat16"), "tb": ("sbuf", [128, 4 * B], "bfloat16"),
+    "a_s": ("sbuf", [128, 4 * A], "bfloat16"), "b_s": ("sbuf", [128, 4 * B], "bfloat16"),
     "y_s": ("sbuf", [128, B], "float32"),
     "cxa": ("sbuf", [128, A], CODE), "pxa": ("sbuf", [128, A], PLANE),
     "cxb": ("sbuf", [128, B], CODE), "pxb": ("sbuf", [128, B], PLANE),
@@ -19,13 +27,13 @@ SCRATCH = {
     "cra": ("sbuf", [128, A], CODE), "pra": ("sbuf", [128, A], PLANE),
     "crb": ("sbuf", [128, B], CODE), "prb": ("sbuf", [128, B], PLANE),
 }
-for _i in range(G):
-    SCRATCH["zb%d" % _i] = ("psum", [128, 512], "float32")
-    SCRATCH["za%d" % _i] = ("psum", [128, 512], "float32")
+for _i in range(8):
+    SCRATCH["z%d" % _i] = ("psum", [128, 512], "float32")
 
-SEMAPHORES = ["l_xa", "l_xb", "l_wa0", "l_wa1", "l_wb0", "l_wb1", "q_xa", "q_xb", "q_a", "q_b",
-              "arr_a", "arr_b", "sent", "y0", "y1", "yv", "ys", "stored"]
-SEMAPHORES += ["%s%d" % (n, i) for n in ("q_wa", "q_wb", "m_a", "m_b", "r_a", "r_b") for i in range(G)]
+SEMAPHORES = ["arr_a", "arr_b", "sent", "y0", "y1", "yv", "ys", "stored0", "stored1"]
+SEMAPHORES += ["l_%s%d" % (n, i) for n in PIECES for i in range(len(PIECES[n]) - 1)]
+SEMAPHORES += ["q_%s%d" % o for o in ORDER]
+SEMAPHORES += ["%s%d" % (n, i) for n in ("m", "r") for i in range(len(PRODUCTS))]
 
 
 def rank_program(g, core, T, topo):
@@ -37,72 +45,76 @@ def rank_program(g, core, T, topo):
     row_peer = T.cores[2 * i + (1 - j)]
     col_peer = T.cores[2 * (1 - i) + j]
     Relu, Copy = ActivationFunctionType.Relu, ActivationFunctionType.Copy
-    cut = 3 * 512
+    queues = {"sync": g.sync, "scalar": g.scalar}
 
-    g.sync.dma_start(T.xb_s[:], T.xb[:]).then_inc(S.l_xb, 16)
-    g.scalar.dma_start(T.wb_s[:, :cut], T.wb[:, :cut]).then_inc(S.l_wb0, 16)
-    g.sync.dma_start(T.wb_s[:, cut:], T.wb[:, cut:]).then_inc(S.l_wb1, 16)
-    g.scalar.dma_start(T.wa_s[:, :cut], T.wa[:, :cut]).then_inc(S.l_wa0, 16)
-    g.sync.dma_start(T.xa_s[:], T.xa[:]).then_inc(S.l_xa, 16)
-    g.sync.dma_start(T.wa_s[:, cut:], T.wa[:, cut:]).then_inc(S.l_wa1, 16)
+    for queue, name, piece in LOADS:
+        c = slice(512 * PIECES[name][piece], 512 * PIECES[name][piece + 1])
+        queues[queue].dma_start(T[name + "_s"][:, c], T[name][:, c]).then_inc(S["l_%s%d" % (name, piece)], 16)
 
-    for t, n in (("b", B), ("a", A)):
-        x, w, cx, px = T["x%s_s" % t], T["w%s_s" % t], T["cx" + t], T["px" + t]
-        cw, pw, h = T["cw" + t], T["pw" + t], T["t" + t]
-        g.vector.wait_ge(S["l_x" + t], 16)
-        g.vector.quantize_mx(cx[:], px[:], x[:]).then_inc(S["q_x" + t], 1)
-        g.tensor.wait_ge(S["q_x" + t], 1)
-        for b in range(G):
-            if b == 0:
-                g.vector.wait_ge(S["l_w%s0" % t], 16)
-            if b == G - 1:
-                g.vector.wait_ge(S["l_w%s1" % t], 16)
-            c = slice(128 * b, 128 * b + 128)
-            g.vector.quantize_mx(cw[:, c], pw[:, c], w[:, 512 * b:512 * b + 512]).then_inc(S["q_w%s%d" % (t, b)], 1)
-            z = T["z%s%d" % (t, b)]
-            g.tensor.wait_ge(S["q_w%s%d" % (t, b)], 1)
-            g.tensor.matmul_mx(z[:, :n], cw[:, c], pw[:, c], cx[:], px[:], True, True).then_inc(S["m_%s%d" % (t, b)], 1)
-            if b < G - 1:
-                g.scalar.wait_ge(S["m_%s%d" % (t, b)], 1)
-                g.scalar.activation(h[:, b:4 * n:4], z[:, :n], Relu, scale=C).then_inc(S["r_%s%d" % (t, b)], 1)
-            else:
-                g.vector.wait_ge(S["m_%s%d" % (t, b)], 1)
-                g.vector.tensor_scalar(h[:, b:4 * n:4], z[:, :n], 0.0, C, AluOpType.max, AluOpType.mult).then_inc(
-                    S["r_%s%d" % (t, b)], 1)
-        for b in range(G):
-            g.vector.wait_ge(S["r_%s%d" % (t, b)], 1)
-        g.vector.quantize_mx(T["c" + t][:], T["p" + t][:], h[:]).then_inc(S["q_" + t], 1)
+    for name, block in ORDER:
+        if name in PIECES:
+            if block in PIECES[name]:
+                g.vector.wait_ge(S["l_%s%d" % (name, PIECES[name].index(block))], 16)
+        else:
+            for p, (tile, _, half, _) in enumerate(PRODUCTS):
+                if (tile, half) == (name, block):
+                    g.vector.wait_ge(S["r%d" % p], 1)
+        c = slice(128 * block, 128 * block + 128)
+        g.vector.quantize_mx(T["c" + name][:, c], T["p" + name][:, c], T[name + "_s"][:, 512 * block:512 * block + 512]).then_inc(
+            S["q_%s%d" % (name, block)], 1)
 
-    eng_b = topo.mask(core, col_peer)
-    eng_a = topo.mask(core, row_peer) & eng_b
+    last = {}
+    seen = set()
+    for p, (t, b, half, bank) in enumerate(PRODUCTS):
+        c, x = slice(128 * b, 128 * b + 128), slice(H * half, H * half + H)
+        need = ["q_x%s%d" % (t, half), "q_w%s%d" % (t, b)] + (["r%d" % last[bank]] if bank in last else [])
+        for s in need:
+            if s not in seen:
+                seen.add(s)
+                g.tensor.wait_ge(S[s], 1)
+        last[bank] = p
+        z = T["z%d" % bank][:, :H]
+        g.tensor.matmul_mx(z, T["cw" + t][:, c], T["pw" + t][:, c], T["cx" + t][:, x], T["px" + t][:, x], True, True).then_inc(
+            S["m%d" % p], 1)
+        g.scalar.wait_ge(S["m%d" % p], 1)
+        g.scalar.activation(T[t + "_s"][:, 512 * half + b:512 * half + 512:4], z, Relu, scale=C).then_inc(S["r%d" % p], 1)
+
+    eng_b, eng_a = topo.mask(core, col_peer), topo.mask(core, row_peer)
     n_a, n_b = bin(eng_a).count("1"), bin(eng_b).count("1")
-    for t, dst, eng in (("b", col_peer, eng_b), ("a", row_peer, eng_a)):
-        rid, pid = topo.addr(dst, core)
-        g.wait_ge(S["q_" + t], 1)
-        g.remote_dma(T["cr" + t][:].bitcast(dt.uint8), T["c" + t][:].bitcast(dt.uint8), S["arr_" + t], S.sent, pid, rid, eng)
-        g.remote_dma(T["pr" + t][:], T["p" + t][:], S["arr_" + t], S.sent, pid, rid, eng)
+    rid, pid = topo.addr(col_peer, core)
+    for h in range(2):
+        c = slice(H * h, H * h + H)
+        g.wait_ge(S["q_b%d" % h], 1)
+        g.remote_dma(T.crb[:, c].bitcast(dt.uint8), T.cb[:, c].bitcast(dt.uint8), S.arr_b, S.sent, pid, rid, eng_b)
+    g.remote_dma(T.prb[:], T.pb[:], S.arr_b, S.sent, pid, rid, eng_b)
+    rid, pid = topo.addr(row_peer, core)
+    g.wait_ge(S.q_a0, 1)
+    g.remote_dma(T.cra[:].bitcast(dt.uint8), T.ca[:].bitcast(dt.uint8), S.arr_a, S.sent, pid, rid, eng_a)
+    g.remote_dma(T.pra[:], T.pa[:], S.arr_a, S.sent, pid, rid, eng_a)
 
     own_a, rem_a = (T.ca, T.pa), (T.cra, T.pra)
     own_b, rem_b = (T.cb, T.pb), (T.crb, T.prb)
     slices = ((own_a, own_b), (rem_a, rem_b)) if i == j else ((own_a, rem_b), (rem_a, own_b))
-    g.tensor.wait_ge(S.q_b, 1)
-    g.tensor.wait_ge(S.q_a, 1)
+    for s in ("q_b0", "q_b1", "q_a0"):
+        g.tensor.wait_ge(S[s], 1)
     for k, (a, b) in enumerate(slices):
         if b is rem_b:
-            g.tensor.wait_ge(S.arr_b, 2 * n_b)
+            g.tensor.wait_ge(S.arr_b, 3 * n_b)
         if a is rem_a:
             g.tensor.wait_ge(S.arr_a, 2 * n_a)
         for h in range(2):
-            c = slice(128 * h, 128 * h + 128)
-            mm = g.tensor.matmul_mx(T["zb%d" % h][:, :128], a[0][:], a[1][:], b[0][:, c], b[1][:, c], k == 0, k == 1)
+            c = slice(H * h, H * h + H)
+            mm = g.tensor.matmul_mx(T["z%d" % h][:, :H], a[0][:], a[1][:], b[0][:, c], b[1][:, c], k == 0, k == 1)
             if k == 1:
                 mm.then_inc(S["y%d" % h], 1)
     g.vector.wait_ge(S.y0, 1)
-    g.vector.tensor_copy(T.y_s[:, :128], T.zb0[:, :128]).then_inc(S.yv, 1)
+    g.vector.tensor_copy(T.y_s[:, :H], T.z0[:, :H]).then_inc(S.yv, 1)
     g.scalar.wait_ge(S.y1, 1)
-    g.scalar.activation(T.y_s[:, 128:], T.zb1[:, :128], Copy).then_inc(S.ys, 1)
+    g.scalar.activation(T.y_s[:, H:], T.z1[:, :H], Copy).then_inc(S.ys, 1)
     g.sync.wait_ge(S.yv, 1)
-    g.sync.wait_ge(S.ys, 1)
-    g.sync.dma_start(T.y[:], T.y_s[:]).then_inc(S.stored, 16)
-    g.sync.wait_ge(S.stored, 16)
-    g.wait_ge(S.sent, 2 * n_a + 2 * n_b)
+    g.sync.dma_start(T.y[:, :H], T.y_s[:, :H]).then_inc(S.stored0, 16)
+    g.scalar.wait_ge(S.ys, 1)
+    g.scalar.dma_start(T.y[:, H:], T.y_s[:, H:]).then_inc(S.stored1, 16)
+    g.sync.wait_ge(S.stored0, 16)
+    g.scalar.wait_ge(S.stored1, 16)
+    g.wait_ge(S.sent, 2 * n_a + 3 * n_b)

from concourse.mybir import ActivationFunctionType, dt

CODE, PLANE = "float8_e4m3fn_x4", "uint8"
C = 0.041
G = 4
A, B, H = 128, 256, 128
PIECES = {"xa": (0, 1), "xb": (0, 1, 2), "wa": (0, 1, 3, 4), "wb": (0, 2, 3, 4)}
LOADS = (("sync", "xb", 0), ("scalar", "wb", 0), ("sync", "wb", 1), ("scalar", "wb", 2), ("sync", "xb", 1),
         ("scalar", "xa", 0), ("sync", "wa", 0), ("scalar", "wa", 1), ("sync", "wa", 2))
ORDER = (("xb", 0), ("wb", 0), ("wb", 1), ("wb", 2), ("wb", 3), ("xb", 1), ("b", 0), ("xa", 0), ("wa", 0), ("b", 1),
         ("wa", 1), ("wa", 2), ("wa", 3), ("a", 0))
PRODUCTS = (("b", 0, 0, 0), ("b", 1, 0, 1), ("b", 2, 0, 2), ("b", 3, 0, 3),
            ("b", 0, 1, 4), ("b", 1, 1, 5), ("b", 2, 1, 6), ("b", 3, 1, 7),
            ("a", 0, 0, 0), ("a", 1, 0, 1), ("a", 2, 0, 2), ("a", 3, 0, 3))

SCRATCH = {
    "xa_s": ("sbuf", [128, 4 * A], "bfloat16"), "xb_s": ("sbuf", [128, 4 * B], "bfloat16"),
    "wa_s": ("sbuf", [128, G * 512], "bfloat16"), "wb_s": ("sbuf", [128, G * 512], "bfloat16"),
    "a_s": ("sbuf", [128, 4 * A], "bfloat16"), "b_s": ("sbuf", [128, 4 * B], "bfloat16"),
    "y_s": ("sbuf", [128, B], "float32"),
    "cxa": ("sbuf", [128, A], CODE), "pxa": ("sbuf", [128, A], PLANE),
    "cxb": ("sbuf", [128, B], CODE), "pxb": ("sbuf", [128, B], PLANE),
    "cwa": ("sbuf", [128, G * 128], CODE), "pwa": ("sbuf", [128, G * 128], PLANE),
    "cwb": ("sbuf", [128, G * 128], CODE), "pwb": ("sbuf", [128, G * 128], PLANE),
    "ca": ("sbuf", [128, A], CODE), "pa": ("sbuf", [128, A], PLANE),
    "cb": ("sbuf", [128, B], CODE), "pb": ("sbuf", [128, B], PLANE),
    "cra": ("sbuf", [128, A], CODE), "pra": ("sbuf", [128, A], PLANE),
    "crb": ("sbuf", [128, B], CODE), "prb": ("sbuf", [128, B], PLANE),
}
for _i in range(8):
    SCRATCH["z%d" % _i] = ("psum", [128, 512], "float32")

SEMAPHORES = ["arr_a", "arr_b", "sent", "y0", "y1", "yv", "ys", "stored0", "stored1"]
SEMAPHORES += ["l_%s%d" % (n, i) for n in PIECES for i in range(len(PIECES[n]) - 1)]
SEMAPHORES += ["q_%s%d" % o for o in ORDER]
SEMAPHORES += ["%s%d" % (n, i) for n in ("m", "r") for i in range(len(PRODUCTS))]


def rank_program(g, core, T, topo):
    rank = T.rank_of(core)
    if rank is None:
        return
    S = T.sem
    i, j = divmod(rank, 2)
    row_peer = T.cores[2 * i + (1 - j)]
    col_peer = T.cores[2 * (1 - i) + j]
    Relu, Copy = ActivationFunctionType.Relu, ActivationFunctionType.Copy
    queues = {"sync": g.sync, "scalar": g.scalar}

    for queue, name, piece in LOADS:
        c = slice(512 * PIECES[name][piece], 512 * PIECES[name][piece + 1])
        queues[queue].dma_start(T[name + "_s"][:, c], T[name][:, c]).then_inc(S["l_%s%d" % (name, piece)], 16)

    for name, block in ORDER:
        if name in PIECES:
            if block in PIECES[name]:
                g.vector.wait_ge(S["l_%s%d" % (name, PIECES[name].index(block))], 16)
        else:
            for p, (tile, _, half, _) in enumerate(PRODUCTS):
                if (tile, half) == (name, block):
                    g.vector.wait_ge(S["r%d" % p], 1)
        c = slice(128 * block, 128 * block + 128)
        g.vector.quantize_mx(T["c" + name][:, c], T["p" + name][:, c], T[name + "_s"][:, 512 * block:512 * block + 512]).then_inc(
            S["q_%s%d" % (name, block)], 1)

    last = {}
    seen = set()
    for p, (t, b, half, bank) in enumerate(PRODUCTS):
        c, x = slice(128 * b, 128 * b + 128), slice(H * half, H * half + H)
        need = ["q_x%s%d" % (t, half), "q_w%s%d" % (t, b)] + (["r%d" % last[bank]] if bank in last else [])
        for s in need:
            if s not in seen:
                seen.add(s)
                g.tensor.wait_ge(S[s], 1)
        last[bank] = p
        z = T["z%d" % bank][:, :H]
        g.tensor.matmul_mx(z, T["cw" + t][:, c], T["pw" + t][:, c], T["cx" + t][:, x], T["px" + t][:, x], True, True).then_inc(
            S["m%d" % p], 1)
        g.scalar.wait_ge(S["m%d" % p], 1)
        g.scalar.activation(T[t + "_s"][:, 512 * half + b:512 * half + 512:4], z, Relu, scale=C).then_inc(S["r%d" % p], 1)

    eng_b, eng_a = topo.mask(core, col_peer), topo.mask(core, row_peer)
    n_a, n_b = bin(eng_a).count("1"), bin(eng_b).count("1")
    rid, pid = topo.addr(col_peer, core)
    for h in range(2):
        c = slice(H * h, H * h + H)
        g.wait_ge(S["q_b%d" % h], 1)
        g.remote_dma(T.crb[:, c].bitcast(dt.uint8), T.cb[:, c].bitcast(dt.uint8), S.arr_b, S.sent, pid, rid, eng_b)
    g.remote_dma(T.prb[:], T.pb[:], S.arr_b, S.sent, pid, rid, eng_b)
    rid, pid = topo.addr(row_peer, core)
    g.wait_ge(S.q_a0, 1)
    g.remote_dma(T.cra[:].bitcast(dt.uint8), T.ca[:].bitcast(dt.uint8), S.arr_a, S.sent, pid, rid, eng_a)
    g.remote_dma(T.pra[:], T.pa[:], S.arr_a, S.sent, pid, rid, eng_a)

    own_a, rem_a = (T.ca, T.pa), (T.cra, T.pra)
    own_b, rem_b = (T.cb, T.pb), (T.crb, T.prb)
    slices = ((own_a, own_b), (rem_a, rem_b)) if i == j else ((own_a, rem_b), (rem_a, own_b))
    for s in ("q_b0", "q_b1", "q_a0"):
        g.tensor.wait_ge(S[s], 1)
    for k, (a, b) in enumerate(slices):
        if b is rem_b:
            g.tensor.wait_ge(S.arr_b, 3 * n_b)
        if a is rem_a:
            g.tensor.wait_ge(S.arr_a, 2 * n_a)
        for h in range(2):
            c = slice(H * h, H * h + H)
            mm = g.tensor.matmul_mx(T["z%d" % h][:, :H], a[0][:], a[1][:], b[0][:, c], b[1][:, c], k == 0, k == 1)
            if k == 1:
                mm.then_inc(S["y%d" % h], 1)
    g.vector.wait_ge(S.y0, 1)
    g.vector.tensor_copy(T.y_s[:, :H], T.z0[:, :H]).then_inc(S.yv, 1)
    g.scalar.wait_ge(S.y1, 1)
    g.scalar.activation(T.y_s[:, H:], T.z1[:, :H], Copy).then_inc(S.ys, 1)
    g.sync.wait_ge(S.yv, 1)
    g.sync.dma_start(T.y[:, :H], T.y_s[:, :H]).then_inc(S.stored0, 16)
    g.scalar.wait_ge(S.ys, 1)
    g.scalar.dma_start(T.y[:, H:], T.y_s[:, H:]).then_inc(S.stored1, 16)
    g.sync.wait_ge(S.stored0, 16)
    g.scalar.wait_ge(S.stored1, 16)
    g.wait_ge(S.sent, 2 * n_a + 3 * n_b)
